import numpy as np
CORES = [0,8,16,24,32,40,48,56,64,72,80,88,96,104,112,120]
N = 16
ROOT = 1
WIDTHS = [1,1,1,1,1,1,4,1,1,1,1,4,4,4,1,4]
XW = 4
def setup_inputs(rng):
    return {"x": rng.standard_normal((N, 128, XW), dtype=np.float32)}
def reference(x):
    g = np.concatenate([x[r][:, :WIDTHS[r]] for r in range(N)], axis=1)
    y = np.full((N, 128, g.shape[1]), np.nan, x.dtype)
    y[ROOT] = g
    return {"y": y}

XW = 4
YW = 31
RELAY = 2

SCRATCH = {
    "xd": ("dram", [128, XW], "float32"),
    "xs": ("sbuf", [128, XW], "float32"),
    "land": ("sbuf", [128, YW], "float32"),
}
SEMAPHORES = ["loaded", "hop", "arrived", "sent", "stored"]


def _bits(m):
    return bin(m).count("1")


def _send(g, T, topo, src, dst, out_ap, in_ap, remote_sem):
    rid, pid, _se = topo.addr(dst)
    m = topo.mask(src, dst)
    g.remote_dma(out_ap, in_ap, remote_sem, T.sem.sent, pid, rid, m)
    g.wait_ge(T.sem.sent, _bits(m))


def rank_program(g, core, T, topo):
    widths = T.tables["WIDTHS"]
    cores = list(T.cores)
    root_rank = 1
    root = cores[root_rank]
    offs = [sum(widths[:r]) for r in range(len(widths))]

    rank = T.rank_of(core)

    if core == root:
        s = g.sync
        w, off = widths[rank], offs[rank]
        s.dma_start(T.xs[:], T.x[:]).then_inc(T.sem.loaded, 16)
        s.wait_ge(T.sem.loaded, 16)
        s.dma_start(T.land[:, off:off + w], T.xs[:, 0:w]).then_inc(T.sem.arrived, 16)
        total = 16
        for r, c in enumerate(cores):
            if c == root:
                continue
            last = c if topo.may_write(c, root) else c + RELAY
            total += _bits(topo.mask(last, root))
        s.wait_ge(T.sem.arrived, total)
        s.dma_start(T.y[:], T.land[:]).then_inc(T.sem.stored, 16)
        s.wait_ge(T.sem.stored, 16)
        return

    if rank is not None:
        w, off = widths[rank], offs[rank]
        direct = topo.may_write(core, root)
        if direct and w < XW:
            g.sync.dma_start(T.xs[:], T.x[:]).then_inc(T.sem.loaded, 16)
            g.wait_ge(T.sem.loaded, 16)
            _send(g, T, topo, core, root, T.land[:, off:off + w], T.xs[:, 0:w], T.sem.arrived)
            return
        g.sync.dma_start(T.xd[:], T.x[:]).then_inc(T.sem.loaded, 16)
        g.wait_ge(T.sem.loaded, 16)
        if direct:
            _send(g, T, topo, core, root, T.land[:, off:off + w], T.xd[:], T.sem.arrived)
        elif w < XW:
            _send(g, T, topo, core, core + RELAY, T.xs[:], T.xd[:], T.sem.hop)
        else:
            _send(g, T, topo, core, core + RELAY, T.xd[:], T.xd[:], T.sem.hop)
        return

    owner = core - RELAY
    if owner in cores and owner != root and not topo.may_write(owner, root):
        r = cores.index(owner)
        w, off = widths[r], offs[r]
        g.wait_ge(T.sem.hop, _bits(topo.mask(owner, core)))
        src = T.xs[:, 0:w] if w < XW else T.xd[:]
        _send(g, T, topo, core, root, T.land[:, off:off + w], src, T.sem.arrived)
